import numpy as np
import ml_dtypes

BF16 = ml_dtypes.bfloat16


def bf(x):
    return np.asarray(x, np.float32).astype(BF16)


def f32(x):
    return np.asarray(x, np.float32)


def f64(x):
    return np.asarray(x).astype(np.float64)


def striped(idx):
    return np.concatenate([l.reshape(-1, 16).T for l in idx])


def rows(idx, k):
    return np.tile(np.repeat(idx, 16, axis=0), (k // (16 * 8), 1))


def look(tab, idx):
    return np.take_along_axis(f64(tab), rows(idx, len(tab)), axis=1)


P, K, S, V, N = 128, 256, 2048, 1536, 1536


def setup_inputs():
    return {"tab": f32(np.random.standard_normal((2, K, S))), "q": f32(0.5 * np.random.standard_normal((K, 1))), "e": bf(np.repeat(np.eye(8), 16, axis=0)), "et": bf(np.repeat(np.eye(8), 16, axis=0).T), "offs": striped(np.stack([np.random.permutation(S)[:N] for _ in range(8)]))}


def reference(tab, q, e, et, offs):
    idx = np.stack([g.T.reshape(-1) for g in np.split(offs, 8)])
    k = f64(q) * look(tab[0], idx)
    s = np.concatenate([f64(e).T @ k[a:a + P] for a in range(0, K, P)])
    p = 1.0 / (1.0 + np.exp(-s)) / V
    p = np.concatenate([f64(et).T @ p[a:a + 8] for a in range(0, len(p), 8)])
    x = (p * look(tab[1], idx)).sum(axis=1).reshape(-1, P)
    return x

@@ -1,0 +1,91 @@
+import concourse.mybir as mybir
+from concourse.masks import make_identity
+
+BF16, F32, U16 = mybir.dt.bfloat16, mybir.dt.float32, mybir.dt.uint16
+ADD, MULT = mybir.AluOpType.add, mybir.AluOpType.mult
+COPY = mybir.ActivationFunctionType.Copy
+SIGMOID = mybir.ActivationFunctionType.Sigmoid
+
+P = 128
+ROWS, PLACES = 256, 2048
+BLOCKS = ROWS // P
+HEADS = 8
+N = 1536
+PIECE = 512
+PIECES = N // PIECE
+
+FLOPS = 2 * ROWS * N + 2 * HEADS * ROWS * N + 2 * ROWS * N
+
+
+def tile_lookup_hattn_sig_out_kernel(tc, tab, q, e, et, offs, out):
+    nc = tc.nc
+    with (
+        tc.tile_pool(name="held", bufs=1) as held,
+        tc.tile_pool(name="work", bufs=3) as work,
+        tc.psum_pool(name="psum", bufs=2) as psum,
+        tc.psum_pool(name="psum_out", bufs=1) as psum_out,
+    ):
+        offsets = held.tile([P, N // 16], U16, name="offsets")
+        nc.sync.dma_start(offsets[:], offs)
+        q_columns = held.tile([P, BLOCKS], F32, name="q_columns")
+        nc.scalar.dma_start(q_columns[:], q.rearrange("(b p) o -> p (b o)", p=P))
+        keys, values = [], []
+        for b in range(BLOCKS):
+            window = held.tile([P, PLACES], F32, name=f"keys_{b}")
+            nc.sync.dma_start(window[:], tab[0, b * P : (b + 1) * P, :])
+            keys.append(window)
+        sum_rows = held.tile([P, HEADS], BF16, name="sum_rows")
+        nc.scalar.dma_start(sum_rows[:], e)
+        spread_heads = held.tile([HEADS, P], BF16, name="spread_heads")
+        nc.scalar.dma_start(spread_heads[:], et)
+        for b in range(BLOCKS):
+            window = held.tile([P, PLACES], F32, name=f"values_{b}")
+            nc.sync.dma_start(window[:], tab[1, b * P : (b + 1) * P, :])
+            values.append(window)
+
+        zero = held.tile([P, 1], F32, name="zero")
+        nc.vector.memset(zero[:], 0.0)
+        identity = held.tile([P, P], F32, name="identity")
+        make_identity(nc, identity[:])
+
+        def list_piece(i):
+            return offsets[:, i * PIECE // 16 : (i + 1) * PIECE // 16]
+
+        weights = {}
+        for b in range(BLOCKS):
+            for i in range(PIECES):
+                key_q = work.tile([P, PIECE], F32, name="key_q")
+                nc.vector.tensor_scalar(
+                    key_q[:], keys[b][:].indirect(list_piece(i)), q_columns[:, b : b + 1], zero[:], MULT, ADD
+                )
+                key_q_bf = work.tile([P, PIECE], BF16, name="key_q_bf")
+                nc.scalar.copy(key_q_bf[:], key_q[:])
+                scores = psum.tile([HEADS, PIECE], F32, name="scores")
+                nc.tensor.matmul(scores[:], sum_rows[:], key_q_bf[:], start=True, stop=True)
+                sigmoids = work.tile([HEADS, PIECE], BF16, name="sigmoids")
+                nc.scalar.activation(sigmoids[:], scores[:], SIGMOID)
+                spread = psum.tile([P, PIECE], F32, name="spread")
+                nc.tensor.matmul(spread[:], spread_heads[:], sigmoids[:], start=True, stop=True)
+                weight = held.tile([P, PIECE], F32, name=f"weight_{b}_{i}")
+                nc.scalar.copy(weight[:], spread[:])
+                weights[b, i] = weight
+
+        partial = held.tile([P, PIECES * BLOCKS], F32, name="partial")
+        for b in range(BLOCKS):
+            for i in range(PIECES):
+                weighted = work.tile([P, PIECE], F32, name="weighted")
+                nc.vector.tensor_tensor(weighted[:], values[b][:].indirect(list_piece(i)), weights[b, i][:], MULT)
+                scaled = work.tile([P, PIECE], F32, name="scaled")
+                column = i * BLOCKS + b
+                nc.scalar.activation(
+                    scaled[:], weighted[:], COPY, scale=1.0 / N, accum_out=partial[:, column : column + 1]
+                )
+
+        rows = psum_out.tile([BLOCKS, P], F32, name="rows")
+        for i in range(PIECES):
+            nc.tensor.matmul(
+                rows[:], partial[:, i * BLOCKS : (i + 1) * BLOCKS], identity[:], start=i == 0, stop=i == PIECES - 1
+            )
+        result = held.tile([BLOCKS, P], F32, name="result")
+        nc.vector.tensor_copy(result[:], rows[:])
+        nc.sync.dma_start(out, result[:])

@@ -14,7 +14,7 @@ N = 1536
 PIECE = 512
 PIECES = N // PIECE
 
-FLOPS = 2 * ROWS * N + 2 * HEADS * ROWS * N + 2 * ROWS * N
+FLOPS = ROWS * N + 2 * P * ROWS * N + 2 * ROWS * N
 
 
 def tile_lookup_hattn_sig_out_kernel(tc, tab, q, e, et, offs, out):
@@ -22,11 +22,13 @@ def tile_lookup_hattn_sig_out_kernel(tc, tab, q, e, et, offs, out):
     with (
         tc.tile_pool(name="held", bufs=1) as held,
         tc.tile_pool(name="work", bufs=3) as work,
-        tc.psum_pool(name="psum", bufs=2) as psum,
-        tc.psum_pool(name="psum_out", bufs=1) as psum_out,
+        tc.psum_pool(name="psum", bufs=4) as psum,
+        tc.psum_pool(name="psum_once", bufs=1) as psum_once,
     ):
         offsets = held.tile([P, N // 16], U16, name="offsets")
         nc.sync.dma_start(offsets[:], offs)
+        spread_heads = held.tile([HEADS, P], BF16, name="spread_heads")
+        nc.scalar.dma_start(spread_heads[:], et)
         q_columns = held.tile([P, BLOCKS], F32, name="q_columns")
         nc.scalar.dma_start(q_columns[:], q.rearrange("(b p) o -> p (b o)", p=P))
         keys, values = [], []
@@ -34,10 +36,6 @@ def tile_lookup_hattn_sig_out_kernel(tc, tab, q, e, et, offs, out):
             window = held.tile([P, PLACES], F32, name=f"keys_{b}")
             nc.sync.dma_start(window[:], tab[0, b * P : (b + 1) * P, :])
             keys.append(window)
-        sum_rows = held.tile([P, HEADS], BF16, name="sum_rows")
-        nc.scalar.dma_start(sum_rows[:], e)
-        spread_heads = held.tile([HEADS, P], BF16, name="spread_heads")
-        nc.scalar.dma_start(spread_heads[:], et)
         for b in range(BLOCKS):
             window = held.tile([P, PLACES], F32, name=f"values_{b}")
             nc.sync.dma_start(window[:], tab[1, b * P : (b + 1) * P, :])
@@ -47,6 +45,11 @@ def tile_lookup_hattn_sig_out_kernel(tc, tab, q, e, et, offs, out):
         nc.vector.memset(zero[:], 0.0)
         identity = held.tile([P, P], F32, name="identity")
         make_identity(nc, identity[:])
+
+        same_head_sums = psum_once.tile([P, P], F32, name="same_head_sums")
+        nc.tensor.matmul(same_head_sums[:], spread_heads[:], spread_heads[:], start=True, stop=True)
+        same_head = held.tile([P, P], F32, name="same_head")
+        nc.vector.tensor_copy(same_head[:], same_head_sums[:])
 
         def list_piece(i):
             return offsets[:, i * PIECE // 16 : (i + 1) * PIECE // 16]
@@ -58,16 +61,10 @@ def tile_lookup_hattn_sig_out_kernel(tc, tab, q, e, et, offs, out):
                 nc.vector.tensor_scalar(
                     key_q[:], keys[b][:].indirect(list_piece(i)), q_columns[:, b : b + 1], zero[:], MULT, ADD
                 )
-                key_q_bf = work.tile([P, PIECE], BF16, name="key_q_bf")
-                nc.scalar.copy(key_q_bf[:], key_q[:])
-                scores = psum.tile([HEADS, PIECE], F32, name="scores")
-                nc.tensor.matmul(scores[:], sum_rows[:], key_q_bf[:], start=True, stop=True)
-                sigmoids = work.tile([HEADS, PIECE], BF16, name="sigmoids")
-                nc.scalar.activation(sigmoids[:], scores[:], SIGMOID)
-                spread = psum.tile([P, PIECE], F32, name="spread")
-                nc.tensor.matmul(spread[:], spread_heads[:], sigmoids[:], start=True, stop=True)
+                scores = psum.tile([P, PIECE], F32, name="scores")
+                nc.tensor.matmul(scores[:], same_head[:], key_q[:], start=True, stop=True)
                 weight = held.tile([P, PIECE], F32, name=f"weight_{b}_{i}")
-                nc.scalar.copy(weight[:], spread[:])
+                nc.scalar.activation(weight[:], scores[:], SIGMOID)
                 weights[b, i] = weight
 
         partial = held.tile([P, PIECES * BLOCKS], F32, name="partial")
@@ -81,7 +78,7 @@ def tile_lookup_hattn_sig_out_kernel(tc, tab, q, e, et, offs, out):
                     scaled[:], weighted[:], COPY, scale=1.0 / N, accum_out=partial[:, column : column + 1]
                 )
 
-        rows = psum_out.tile([BLOCKS, P], F32, name="rows")
+        rows = psum_once.tile([BLOCKS, P], F32, name="rows")
         for i in range(PIECES):
             nc.tensor.matmul(
                 rows[:], partial[:, i * BLOCKS : (i + 1) * BLOCKS], identity[:], start=i == 0, stop=i == PIECES - 1

@@ -21,6 +21,7 @@ def tile_lookup_hattn_sig_out_kernel(tc, tab, q, e, et, offs, out):
     nc = tc.nc
     with (
         tc.tile_pool(name="held", bufs=1) as held,
+        tc.tile_pool(name="products", bufs=BLOCKS * PIECES) as products,
         tc.tile_pool(name="work", bufs=3) as work,
         tc.psum_pool(name="psum", bufs=4) as psum,
         tc.psum_pool(name="psum_once", bufs=1) as psum_once,
@@ -51,38 +52,47 @@ def tile_lookup_hattn_sig_out_kernel(tc, tab, q, e, et, offs, out):
         same_head = held.tile([P, P], F32, name="same_head")
         nc.vector.tensor_copy(same_head[:], same_head_sums[:])
 
-        def list_piece(i):
-            return offsets[:, i * PIECE // 16 : (i + 1) * PIECE // 16]
+        def entries(first, last):
+            return offsets[:, first // 16 : last // 16]
 
-        weights = {}
+        weights = []
         for b in range(BLOCKS):
-            for i in range(PIECES):
-                key_q = work.tile([P, PIECE], F32, name="key_q")
+            weight = held.tile([P, N], F32, name=f"weight_{b}")
+            weights.append(weight)
+            for first in range(0, N, PIECE):
+                last = first + PIECE
+                key_q = products.tile([P, PIECE], F32, name="key_q")
                 nc.vector.tensor_scalar(
-                    key_q[:], keys[b][:].indirect(list_piece(i)), q_columns[:, b : b + 1], zero[:], MULT, ADD
+                    key_q[:], keys[b][:].indirect(entries(first, last)), q_columns[:, b : b + 1], zero[:], MULT, ADD
                 )
                 scores = psum.tile([P, PIECE], F32, name="scores")
                 nc.tensor.matmul(scores[:], same_head[:], key_q[:], start=True, stop=True)
-                weight = held.tile([P, PIECE], F32, name=f"weight_{b}_{i}")
-                nc.scalar.activation(weight[:], scores[:], SIGMOID)
-                weights[b, i] = weight
+                nc.scalar.activation(weight[:, first:last], scores[:], SIGMOID)
 
-        partial = held.tile([P, PIECES * BLOCKS], F32, name="partial")
+        cuts = (0, 512, 1024, N)
+        last_first = cuts[-2]
+        last_width = N - last_first
+        totals = held.tile([P, BLOCKS], F32, name="totals")
         for b in range(BLOCKS):
-            for i in range(PIECES):
-                weighted = work.tile([P, PIECE], F32, name="weighted")
-                nc.vector.tensor_tensor(weighted[:], values[b][:].indirect(list_piece(i)), weights[b, i][:], MULT)
-                scaled = work.tile([P, PIECE], F32, name="scaled")
-                column = i * BLOCKS + b
-                nc.scalar.activation(
-                    scaled[:], weighted[:], COPY, scale=1.0 / N, accum_out=partial[:, column : column + 1]
+            closing = held.tile([P, last_width + len(cuts) - 2], F32, name=f"closing_{b}")
+            for i in range(len(cuts) - 2):
+                first, last = cuts[i], cuts[i + 1]
+                weighted = work.tile([P, last - first], F32, name="weighted")
+                nc.vector.tensor_tensor(
+                    weighted[:], values[b][:].indirect(entries(first, last)), weights[b][:, first:last], MULT
                 )
+                copied = work.tile([P, last - first], F32, name="copied")
+                nc.scalar.activation(
+                    copied[:], weighted[:], COPY, accum_out=closing[:, last_width + i : last_width + i + 1]
+                )
+            nc.vector.tensor_tensor(
+                closing[:, :last_width], values[b][:].indirect(entries(last_first, N)), weights[b][:, last_first:], MULT
+            )
+            scaled = work.tile([P, last_width + len(cuts) - 2], F32, name="scaled")
+            nc.scalar.activation(scaled[:], closing[:], COPY, scale=1.0 / N, accum_out=totals[:, b : b + 1])
 
         rows = psum_once.tile([BLOCKS, P], F32, name="rows")
-        for i in range(PIECES):
-            nc.tensor.matmul(
-                rows[:], partial[:, i * BLOCKS : (i + 1) * BLOCKS], identity[:], start=i == 0, stop=i == PIECES - 1
-            )
+        nc.tensor.transpose(rows[:], totals[:], identity[:])
         result = held.tile([BLOCKS, P], F32, name="result")
         nc.vector.tensor_copy(result[:], rows[:])
         nc.sync.dma_start(out, result[:])

@@ -26,12 +26,12 @@ def tile_lookup_hattn_sig_out_kernel(tc, tab, q, e, et, offs, out):
         tc.psum_pool(name="psum", bufs=4) as psum,
         tc.psum_pool(name="psum_once", bufs=1) as psum_once,
     ):
+        q_rows = held.tile([BLOCKS, P], F32, name="q_rows")
+        nc.sync.dma_start(q_rows[:], q.rearrange("(b p) o -> b (p o)", p=P))
         offsets = held.tile([P, N // 16], U16, name="offsets")
         nc.sync.dma_start(offsets[:], offs)
         spread_heads = held.tile([HEADS, P], BF16, name="spread_heads")
         nc.scalar.dma_start(spread_heads[:], et)
-        q_columns = held.tile([P, BLOCKS], F32, name="q_columns")
-        nc.scalar.dma_start(q_columns[:], q.rearrange("(b p) o -> p (b o)", p=P))
         keys, values = [], []
         for b in range(BLOCKS):
             window = held.tile([P, PLACES], F32, name=f"keys_{b}")
@@ -46,6 +46,11 @@ def tile_lookup_hattn_sig_out_kernel(tc, tab, q, e, et, offs, out):
         nc.vector.memset(zero[:], 0.0)
         identity = held.tile([P, P], F32, name="identity")
         make_identity(nc, identity[:])
+
+        q_turned = psum_once.tile([P, BLOCKS], F32, name="q_turned")
+        nc.tensor.matmul(q_turned[:], q_rows[:], identity[:BLOCKS, :BLOCKS], start=True, stop=True)
+        q_columns = held.tile([P, BLOCKS], F32, name="q_columns")
+        nc.vector.tensor_copy(q_columns[:], q_turned[:])
 
         same_head_sums = psum_once.tile([P, P], F32, name="same_head_sums")
         nc.tensor.matmul(same_head_sums[:], spread_heads[:], spread_heads[:], start=True, stop=True)

import concourse.mybir as mybir
from concourse.masks import make_identity

BF16, F32, U16 = mybir.dt.bfloat16, mybir.dt.float32, mybir.dt.uint16
ADD, MULT = mybir.AluOpType.add, mybir.AluOpType.mult
COPY = mybir.ActivationFunctionType.Copy
SIGMOID = mybir.ActivationFunctionType.Sigmoid

P = 128
ROWS, PLACES = 256, 2048
BLOCKS = ROWS // P
HEADS = 8
N = 1536
PIECE = 512
PIECES = N // PIECE

FLOPS = ROWS * N + 2 * P * ROWS * N + 2 * ROWS * N


def tile_lookup_hattn_sig_out_kernel(tc, tab, q, e, et, offs, out):
    nc = tc.nc
    with (
        tc.tile_pool(name="held", bufs=1) as held,
        tc.tile_pool(name="products", bufs=BLOCKS * PIECES) as products,
        tc.tile_pool(name="work", bufs=3) as work,
        tc.psum_pool(name="psum", bufs=4) as psum,
        tc.psum_pool(name="psum_once", bufs=1) as psum_once,
    ):
        q_rows = held.tile([BLOCKS, P], F32, name="q_rows")
        nc.sync.dma_start(q_rows[:], q.rearrange("(b p) o -> b (p o)", p=P))
        offsets = held.tile([P, N // 16], U16, name="offsets")
        nc.sync.dma_start(offsets[:], offs)
        spread_heads = held.tile([HEADS, P], BF16, name="spread_heads")
        nc.scalar.dma_start(spread_heads[:], et)
        keys, values = [], []
        for b in range(BLOCKS):
            window = held.tile([P, PLACES], F32, name=f"keys_{b}")
            nc.sync.dma_start(window[:], tab[0, b * P : (b + 1) * P, :])
            keys.append(window)
        for b in range(BLOCKS):
            window = held.tile([P, PLACES], F32, name=f"values_{b}")
            nc.sync.dma_start(window[:], tab[1, b * P : (b + 1) * P, :])
            values.append(window)

        zero = held.tile([P, 1], F32, name="zero")
        nc.vector.memset(zero[:], 0.0)
        identity = held.tile([P, P], F32, name="identity")
        make_identity(nc, identity[:])

        q_turned = psum_once.tile([P, BLOCKS], F32, name="q_turned")
        nc.tensor.matmul(q_turned[:], q_rows[:], identity[:BLOCKS, :BLOCKS], start=True, stop=True)
        q_columns = held.tile([P, BLOCKS], F32, name="q_columns")
        nc.vector.tensor_copy(q_columns[:], q_turned[:])

        same_head_sums = psum_once.tile([P, P], F32, name="same_head_sums")
        nc.tensor.matmul(same_head_sums[:], spread_heads[:], spread_heads[:], start=True, stop=True)
        same_head = held.tile([P, P], F32, name="same_head")
        nc.vector.tensor_copy(same_head[:], same_head_sums[:])

        def entries(first, last):
            return offsets[:, first // 16 : last // 16]

        weights = []
        for b in range(BLOCKS):
            weight = held.tile([P, N], F32, name=f"weight_{b}")
            weights.append(weight)
            for first in range(0, N, PIECE):
                last = first + PIECE
                key_q = products.tile([P, PIECE], F32, name="key_q")
                nc.vector.tensor_scalar(
                    key_q[:], keys[b][:].indirect(entries(first, last)), q_columns[:, b : b + 1], zero[:], MULT, ADD
                )
                scores = psum.tile([P, PIECE], F32, name="scores")
                nc.tensor.matmul(scores[:], same_head[:], key_q[:], start=True, stop=True)
                nc.scalar.activation(weight[:, first:last], scores[:], SIGMOID)

        cuts = (0, 512, 1024, N)
        last_first = cuts[-2]
        last_width = N - last_first
        totals = held.tile([P, BLOCKS], F32, name="totals")
        for b in range(BLOCKS):
            closing = held.tile([P, last_width + len(cuts) - 2], F32, name=f"closing_{b}")
            for i in range(len(cuts) - 2):
                first, last = cuts[i], cuts[i + 1]
                weighted = work.tile([P, last - first], F32, name="weighted")
                nc.vector.tensor_tensor(
                    weighted[:], values[b][:].indirect(entries(first, last)), weights[b][:, first:last], MULT
                )
                copied = work.tile([P, last - first], F32, name="copied")
                nc.scalar.activation(
                    copied[:], weighted[:], COPY, accum_out=closing[:, last_width + i : last_width + i + 1]
                )
            nc.vector.tensor_tensor(
                closing[:, :last_width], values[b][:].indirect(entries(last_first, N)), weights[b][:, last_first:], MULT
            )
            scaled = work.tile([P, last_width + len(cuts) - 2], F32, name="scaled")
            nc.scalar.activation(scaled[:], closing[:], COPY, scale=1.0 / N, accum_out=totals[:, b : b + 1])

        rows = psum_once.tile([BLOCKS, P], F32, name="rows")
        nc.tensor.transpose(rows[:], totals[:], identity[:])
        result = held.tile([BLOCKS, P], F32, name="result")
        nc.vector.tensor_copy(result[:], rows[:])
        nc.sync.dma_start(out, result[:])
